import numpy as np
import ml_dtypes


def mxq(x, axis, fmt="e4m3"):
    dtype, down = {"e4m3": (ml_dtypes.float8_e4m3fn, 7), "e5m2": (ml_dtypes.float8_e5m2, 14)}[fmt]
    v = np.moveaxis(np.asarray(x, np.float32).astype(ml_dtypes.bfloat16).astype(np.float64), axis, -1)
    blocks = v.reshape(v.shape[:-1] + (-1, 32))
    amax = np.abs(blocks).max(-1, keepdims=True)
    byte = np.maximum(np.where(amax > 0, np.frexp(amax)[1] - 1 + 127, 0) - down, 1)
    scale = np.exp2(byte - 127.0)
    codes = (blocks / scale).astype(np.float32).astype(dtype).astype(np.float64)
    return np.moveaxis((codes * scale).reshape(v.shape), -1, axis)


WIDE = False


def mx_kscale(k):
    if not WIDE:
        return np.ones(k)
    levels = np.array([10, -10, 5, -5, 0])
    if k % 512:
        return np.exp2(np.random.permutation(np.resize(levels, k // 32))).repeat(32)
    a = np.empty((k // 512, 16))
    for p in range(k // 512):
        a[p, :8] = np.random.permutation(np.resize(levels, 8))
        for g in range(8):
            far = levels[np.abs(levels - a[p, g]) >= 10]
            a[p, g + 8] = far[np.random.randint(len(far))]
    return np.exp2(a.ravel()).repeat(32)


def f64(x):
    return np.asarray(x).astype(np.float64)


def striped(idx):
    return np.tile(np.asarray(idx).reshape(-1, 16).T, (8, 1)).astype(np.uint16)


def unstriped(offs):
    return offs[:16].T.reshape(-1).astype(np.int64)


G, K, T, D, M = 128, 8, 2048, 512, 512


def setup_inputs():
    n = np.random.standard_normal
    s = mx_kscale(D)[:, None]
    x = n((D, T)) * s
    idx = np.stack([np.random.permutation(T)[:K] for g in range(G)])
    return {
        "xT": x.astype(np.float32),
        "w": (n((D, M)) / np.sqrt(D) / s).astype(np.float32),
        "bias": (0.3 * n((M, 1))).astype(np.float32),
        "offs": striped(idx.reshape(-1)),
    }


def reference(xT, w, bias, offs):
    x = f64(xT)[:, unstriped(offs)]
    y = (mxq(f64(w), 0, "e4m3").T @ mxq(x, 0, "e4m3")).reshape(M, G, K).max(-1)
    y = y + f64(bias)
    return y

@@ -1,0 +1,157 @@
+from contextlib import ExitStack
+
+import concourse.mybir as mybir
+
+F32 = mybir.dt.float32
+BF16 = mybir.dt.bfloat16
+U32 = mybir.dt.uint32
+U16 = mybir.dt.uint16
+U8 = mybir.dt.uint8
+FP8X4 = mybir.dt.float8_e4m3fn_x4
+COPY = mybir.ActivationFunctionType.Copy
+IDENTITY = mybir.ActivationFunctionType.Identity
+MAX = mybir.AluOpType.max
+AXIS_X = mybir.AxisListType.X
+
+P = 128
+D, T, M, G, K = 512, 2048, 512, 128, 8
+ENTRIES = G * K
+PACK = 4
+HALF = ENTRIES // 2
+G_HALF = HALF // K
+M_TILES = M // P
+
+FLOPS = 2 * D * M * ENTRIES
+
+CHUNKS = [
+    (0, 0, 1024, 0),
+    (0, 1024, 2048, 640),
+    (1, 0, 1024, 0),
+    (1, 1024, 1536, 128),
+    (1, 1536, 2048, 352),
+]
+W_HALVES = 2
+PAIR = 2
+
+
+def tile_attend_edge_bias_kernel(tc, xT, w, bias, offs, out):
+    nc = tc.nc
+    with ExitStack() as ctx:
+        keep = ctx.enter_context(tc.tile_pool(name="keep", bufs=1))
+        psum = ctx.enter_context(tc.psum_pool(name="psum", bufs=1))
+
+        offsets = keep.tile([P, ENTRIES // 16], U16, name="offsets")
+        bias_sb = keep.tile([P, W_HALVES, PAIR], F32, name="bias_sb")
+        warm = keep.tile([P, 8], F32, name="warm")
+        warm_out = keep.tile([P, 8], BF16, name="warm_out")
+
+        x_rows = xT.rearrange("(p u t) c -> u p t c", u=2, t=2)
+        raws = []
+        for i, (u, c0, c1, v) in enumerate(CHUNKS):
+            raw = keep.tile([P, 2, c1 - c0], F32, name="raw%d" % i)
+            nc.sync.dma_start(out=raw[:], in_=x_rows[u, :, :, c0:c1])
+            raws.append(raw)
+            if i == 0:
+                nc.sync.dma_start(offsets[:], offs)
+        w_rows = w.rearrange("(p j) (s m e) -> s p j m e", j=PACK, s=W_HALVES, e=PAIR)
+        w_raws = []
+        for s in range(W_HALVES):
+            w_raw = keep.tile([P, PACK, P, PAIR], F32, name="w_raw%d" % s)
+            nc.sync.dma_start(out=w_raw[:], in_=w_rows[s])
+            w_raws.append(w_raw)
+        nc.sync.dma_start(out=bias_sb[:], in_=bias.rearrange("(s p e) o -> p s (e o)", s=W_HALVES, e=PAIR))
+
+        nc.vector.memset(warm[:], 0.0)
+        nc.scalar.activation(warm_out[:], warm[:], COPY)
+
+        pools_bf = [keep.tile([P, T, 2], BF16, name="pool%d" % u, align_bytes=64) for u in range(2)]
+        gathered = [keep.tile([P, HALF, 2, 2], BF16, name="gathered%d" % h, align_bytes=64) for h in range(2)]
+        codes = [keep.tile([P, HALF], U32, name="codes%d" % h, align_bytes=64) for h in range(2)]
+        scales = [keep.tile([P, HALF], U8, name="scales%d" % h, align_bytes=64) for h in range(2)]
+        w_grouped = [keep.tile([P, PAIR, P, PACK], BF16, name="w_grouped%d" % s, align_bytes=64) for s in range(W_HALVES)]
+        w_codes = [keep.tile([P, M // 2], U32, name="w_codes%d" % s, align_bytes=64) for s in range(W_HALVES)]
+        w_scales = [keep.tile([P, M // 2], U8, name="w_scales%d" % s, align_bytes=64) for s in range(W_HALVES)]
+
+        def cast(i):
+            u, c0, c1, v = CHUNKS[i]
+            n = c1 - c0
+            if n > v:
+                nc.scalar.activation(
+                    pools_bf[u][:, c0 + v : c1, :], raws[i][:, :, v:n].rearrange("p t c -> p c t"), COPY
+                )
+            if v:
+                nc.vector.tensor_copy(
+                    out=pools_bf[u][:, c0 : c0 + v, :], in_=raws[i][:, :, 0:v].rearrange("p t c -> p c t")
+                )
+
+        def gather(u, h):
+            window = pools_bf[u][:].rearrange("p c t -> p (c t)").bitcast(U32)
+            target = gathered[h][:].rearrange("p c u t -> p (c u t)").bitcast(U32).rearrange("p (c u) -> p c u", u=2)
+            a = h * (HALF // 16)
+            nc.vector.tensor_copy(
+                out=target[:, :, u], in_=window.indirect(offsets[:, a : a + HALF // 16])
+            )
+
+        cast(0)
+        cast(1)
+        gather(0, 0)
+        cast(2)
+        gather(0, 1)
+        cast(3)
+        cast(4)
+        for s in range(W_HALVES):
+            nc.scalar.activation(
+                w_grouped[s][:].rearrange("p e m j -> p m j e"),
+                w_raws[s][:].rearrange("p j m e -> p m j e"),
+                COPY,
+            )
+        gather(1, 0)
+        gather(1, 1)
+
+        def quantize_x(h):
+            nc.vector.quantize_mx(
+                out=codes[h][:].bitcast(FP8X4),
+                scales=scales[h][:],
+                in_=gathered[h][:].rearrange("p c u t -> p (c u t)"),
+            )
+
+        def quantize_w(s):
+            nc.vector.quantize_mx(
+                out=w_codes[s][:].bitcast(FP8X4),
+                scales=w_scales[s][:],
+                in_=w_grouped[s][:].rearrange("p e m j -> p (e m j)"),
+            )
+
+        quantize_x(0)
+        quantize_w(0)
+        quantize_x(1)
+        quantize_w(1)
+
+        y_max = keep.tile([P, M_TILES, G], F32, name="y_max")
+        y_out = keep.tile([P, M_TILES, G], F32, name="y_out")
+        out_rows = out.rearrange("(s p e) g -> s p e g", s=W_HALVES, e=PAIR)
+        for t in range(M_TILES):
+            for h in range(2):
+                bank = psum.tile([P, HALF], F32, name="bank%d" % (2 * t + h))
+                s, e = divmod(t, PAIR)
+                m_cols = slice(e * P, (e + 1) * P)
+                nc.tensor.matmul_mx(
+                    out=bank[:],
+                    lhsT=w_codes[s][:, m_cols].bitcast(FP8X4),
+                    lhsT_scale=w_scales[s][:, m_cols],
+                    rhs=codes[h][:].bitcast(FP8X4),
+                    rhs_scale=scales[h][:],
+                    start=True,
+                    stop=True,
+                )
+                nc.vector.tensor_reduce(
+                    out=y_max[:, t, h * G_HALF : (h + 1) * G_HALF],
+                    in_=bank[:].rearrange("p (g k) -> p g k", k=K),
+                    axis=AXIS_X,
+                    op=MAX,
+                )
+            nc.scalar.activation(y_out[:, t, :], y_max[:, t, :], IDENTITY, bias=bias_sb[:, s, e : e + 1])
+            if t == 1:
+                nc.sync.dma_start(out=out_rows[0], in_=y_out[:, 0:2, :])
+            if t > 1:
+                nc.sync.dma_start(out=out_rows[1, :, e, :], in_=y_out[:, t, :])

@@ -24,11 +24,11 @@ M_TILES = M // P
 FLOPS = 2 * D * M * ENTRIES
 
 CHUNKS = [
-    (0, 0, 1024, 0),
-    (0, 1024, 2048, 640),
-    (1, 0, 1024, 0),
-    (1, 1024, 1536, 128),
-    (1, 1536, 2048, 352),
+    (0, 0, 1024, 512),
+    (0, 1024, 2048, 704),
+    (1, 0, 1024, 192),
+    (1, 1024, 1536, 512),
+    (1, 1536, 2048, 400),
 ]
 W_HALVES = 2
 PAIR = 2
@@ -66,6 +66,7 @@ def tile_attend_edge_bias_kernel(tc, xT, w, bias, offs, out):
 
         pools_bf = [keep.tile([P, T, 2], BF16, name="pool%d" % u, align_bytes=64) for u in range(2)]
         gathered = [keep.tile([P, HALF, 2, 2], BF16, name="gathered%d" % h, align_bytes=64) for h in range(2)]
+        plain = keep.tile([P, 2, HALF, 2], BF16, name="plain", align_bytes=64)
         codes = [keep.tile([P, HALF], U32, name="codes%d" % h, align_bytes=64) for h in range(2)]
         scales = [keep.tile([P, HALF], U8, name="scales%d" % h, align_bytes=64) for h in range(2)]
         w_grouped = [keep.tile([P, PAIR, P, PACK], BF16, name="w_grouped%d" % s, align_bytes=64) for s in range(W_HALVES)]
@@ -86,11 +87,13 @@ def tile_attend_edge_bias_kernel(tc, xT, w, bias, offs, out):
 
         def gather(u, h):
             window = pools_bf[u][:].rearrange("p c t -> p (c t)").bitcast(U32)
-            target = gathered[h][:].rearrange("p c u t -> p (c u t)").bitcast(U32).rearrange("p (c u) -> p c u", u=2)
+            if h == 0:
+                words = gathered[0][:].rearrange("p c u t -> p (c u t)").bitcast(U32)
+                target = words.rearrange("p (c u) -> p c u", u=2)[:, :, u]
+            else:
+                target = plain[:, u, :, :].rearrange("p c t -> p (c t)").bitcast(U32)
             a = h * (HALF // 16)
-            nc.vector.tensor_copy(
-                out=target[:, :, u], in_=window.indirect(offsets[:, a : a + HALF // 16])
-            )
+            nc.vector.tensor_copy(out=target, in_=window.indirect(offsets[:, a : a + HALF // 16]))
 
         cast(0)
         cast(1)
@@ -99,14 +102,18 @@ def tile_attend_edge_bias_kernel(tc, xT, w, bias, offs, out):
         gather(0, 1)
         cast(3)
         cast(4)
-        for s in range(W_HALVES):
+        def interleave_w(s):
             nc.scalar.activation(
                 w_grouped[s][:].rearrange("p e m j -> p m j e"),
                 w_raws[s][:].rearrange("p j m e -> p m j e"),
                 COPY,
             )
+
         gather(1, 0)
         gather(1, 1)
+        interleave_w(0)
+        nc.scalar.copy(gathered[1][:], plain[:].rearrange("p u c t -> p c u t"))
+        interleave_w(1)
 
         def quantize_x(h):
             nc.vector.quantize_mx(
@@ -122,36 +129,47 @@ def tile_attend_edge_bias_kernel(tc, xT, w, bias, offs, out):
                 in_=w_grouped[s][:].rearrange("p e m j -> p (e m j)"),
             )
 
-        quantize_x(0)
         quantize_w(0)
+        quantize_x(0)
         quantize_x(1)
         quantize_w(1)
 
         y_max = keep.tile([P, M_TILES, G], F32, name="y_max")
         y_out = keep.tile([P, M_TILES, G], F32, name="y_out")
         out_rows = out.rearrange("(s p e) g -> s p e g", s=W_HALVES, e=PAIR)
-        for t in range(M_TILES):
-            for h in range(2):
-                bank = psum.tile([P, HALF], F32, name="bank%d" % (2 * t + h))
-                s, e = divmod(t, PAIR)
-                m_cols = slice(e * P, (e + 1) * P)
-                nc.tensor.matmul_mx(
-                    out=bank[:],
-                    lhsT=w_codes[s][:, m_cols].bitcast(FP8X4),
-                    lhsT_scale=w_scales[s][:, m_cols],
-                    rhs=codes[h][:].bitcast(FP8X4),
-                    rhs_scale=scales[h][:],
-                    start=True,
-                    stop=True,
-                )
-                nc.vector.tensor_reduce(
-                    out=y_max[:, t, h * G_HALF : (h + 1) * G_HALF],
-                    in_=bank[:].rearrange("p (g k) -> p g k", k=K),
-                    axis=AXIS_X,
-                    op=MAX,
-                )
+        def product(t, h):
+            s, e = divmod(t, PAIR)
+            m_cols = slice(e * P, (e + 1) * P)
+            bank = psum.tile([P, HALF], F32, name="bank%d" % (2 * t + h))
+            nc.tensor.matmul_mx(
+                out=bank[:],
+                lhsT=w_codes[s][:, m_cols].bitcast(FP8X4),
+                lhsT_scale=w_scales[s][:, m_cols],
+                rhs=codes[h][:].bitcast(FP8X4),
+                rhs_scale=scales[h][:],
+                start=True,
+                stop=True,
+            )
+            nc.vector.tensor_reduce(
+                out=y_max[:, t, h * G_HALF : (h + 1) * G_HALF],
+                in_=bank[:].rearrange("p (g k) -> p g k", k=K),
+                axis=AXIS_X,
+                op=MAX,
+            )
+
+        def finish(t):
+            s, e = divmod(t, PAIR)
             nc.scalar.activation(y_out[:, t, :], y_max[:, t, :], IDENTITY, bias=bias_sb[:, s, e : e + 1])
-            if t == 1:
-                nc.sync.dma_start(out=out_rows[0], in_=y_out[:, 0:2, :])
-            if t > 1:
-                nc.sync.dma_start(out=out_rows[1, :, e, :], in_=y_out[:, t, :])
+
+        product(0, 0)
+        product(1, 0)
+        product(0, 1)
+        product(1, 1)
+        finish(0)
+        finish(1)
+        nc.sync.dma_start(out=out_rows[0], in_=y_out[:, 0:2, :])
+        for t in (2, 3):
+            product(t, 0)
+            product(t, 1)
+            finish(t)
+            nc.sync.dma_start(out=out_rows[1, :, t - 2, :], in_=y_out[:, t, :])

@@ -11,27 +11,29 @@ FP8X4 = mybir.dt.float8_e4m3fn_x4
 COPY = mybir.ActivationFunctionType.Copy
 IDENTITY = mybir.ActivationFunctionType.Identity
 MAX = mybir.AluOpType.max
+MULT = mybir.AluOpType.mult
+ADD = mybir.AluOpType.add
 AXIS_X = mybir.AxisListType.X
 
 P = 128
 D, T, M, G, K = 512, 2048, 512, 128, 8
 ENTRIES = G * K
-PACK = 4
+PACK = D // P
 HALF = ENTRIES // 2
+QUARTER = ENTRIES // 4
 G_HALF = HALF // K
 M_TILES = M // P
+LAST = M_TILES - 1
+LANES = 16
 
 FLOPS = 2 * D * M * ENTRIES
 
 CHUNKS = [
-    (0, 0, 1024, 512),
-    (0, 1024, 2048, 704),
-    (1, 0, 1024, 192),
-    (1, 1024, 1536, 512),
-    (1, 1536, 2048, 400),
+    (0, 0, 2048, 1344),
+    (1, 0, 1024, 0),
+    (1, 1024, 1664, 640),
+    (1, 1664, 2048, 288),
 ]
-W_HALVES = 2
-PAIR = 2
 
 
 def tile_attend_edge_bias_kernel(tc, xT, w, bias, offs, out):
@@ -40,136 +42,130 @@ def tile_attend_edge_bias_kernel(tc, xT, w, bias, offs, out):
         keep = ctx.enter_context(tc.tile_pool(name="keep", bufs=1))
         psum = ctx.enter_context(tc.psum_pool(name="psum", bufs=1))
 
-        offsets = keep.tile([P, ENTRIES // 16], U16, name="offsets")
-        bias_sb = keep.tile([P, W_HALVES, PAIR], F32, name="bias_sb")
-        warm = keep.tile([P, 8], F32, name="warm")
-        warm_out = keep.tile([P, 8], BF16, name="warm_out")
-
-        x_rows = xT.rearrange("(p u t) c -> u p t c", u=2, t=2)
-        raws = []
-        for i, (u, c0, c1, v) in enumerate(CHUNKS):
-            raw = keep.tile([P, 2, c1 - c0], F32, name="raw%d" % i)
-            nc.sync.dma_start(out=raw[:], in_=x_rows[u, :, :, c0:c1])
-            raws.append(raw)
+        offsets = keep.tile([P, ENTRIES // LANES], U16, name="offsets")
+        x_rows = xT.rearrange("(p u t) n -> u p t n", u=2, t=2)
+        x_raw = []
+        for i, (u, first, end, by_vector) in enumerate(CHUNKS):
+            raw = keep.tile([P, 2, end - first], F32, name="x_raw%d" % i)
+            nc.sync.dma_start(out=raw[:], in_=x_rows[u, :, :, first:end])
+            x_raw.append(raw)
             if i == 0:
                 nc.sync.dma_start(offsets[:], offs)
-        w_rows = w.rearrange("(p j) (s m e) -> s p j m e", j=PACK, s=W_HALVES, e=PAIR)
-        w_raws = []
-        for s in range(W_HALVES):
-            w_raw = keep.tile([P, PACK, P, PAIR], F32, name="w_raw%d" % s)
-            nc.sync.dma_start(out=w_raw[:], in_=w_rows[s])
-            w_raws.append(w_raw)
-        nc.sync.dma_start(out=bias_sb[:], in_=bias.rearrange("(s p e) o -> p s (e o)", s=W_HALVES, e=PAIR))
+        w_rows = w.rearrange("(p j) (s m e) -> s p j m e", j=PACK, s=2, e=2)
+        w_raw = []
+        for s in range(2):
+            raw = keep.tile([P, PACK, P, 2], F32, name="w_raw%d" % s)
+            nc.sync.dma_start(out=raw[:], in_=w_rows[s])
+            w_raw.append(raw)
+        bias_sb = keep.tile([P, 2, 2], F32, name="bias_sb")
+        nc.sync.dma_start(out=bias_sb[:], in_=bias.rearrange("(s p e) o -> p s (e o)", s=2, e=2))
 
-        nc.vector.memset(warm[:], 0.0)
-        nc.scalar.activation(warm_out[:], warm[:], COPY)
+        zeros = keep.tile([P, 8], F32, name="zeros")
+        zeros_copy = keep.tile([P, 8], BF16, name="zeros_copy")
+        nc.vector.memset(zeros[:], 0.0)
+        nc.scalar.activation(zeros_copy[:], zeros[:], COPY)
 
-        pools_bf = [keep.tile([P, T, 2], BF16, name="pool%d" % u, align_bytes=64) for u in range(2)]
-        gathered = [keep.tile([P, HALF, 2, 2], BF16, name="gathered%d" % h, align_bytes=64) for h in range(2)]
-        plain = keep.tile([P, 2, HALF, 2], BF16, name="plain", align_bytes=64)
-        codes = [keep.tile([P, HALF], U32, name="codes%d" % h, align_bytes=64) for h in range(2)]
-        scales = [keep.tile([P, HALF], U8, name="scales%d" % h, align_bytes=64) for h in range(2)]
-        w_grouped = [keep.tile([P, PAIR, P, PACK], BF16, name="w_grouped%d" % s, align_bytes=64) for s in range(W_HALVES)]
-        w_codes = [keep.tile([P, M // 2], U32, name="w_codes%d" % s, align_bytes=64) for s in range(W_HALVES)]
-        w_scales = [keep.tile([P, M // 2], U8, name="w_scales%d" % s, align_bytes=64) for s in range(W_HALVES)]
+        window = [keep.tile([P, T, 2], BF16, name="window%d" % u, align_bytes=64) for u in range(2)]
+        picked = keep.tile([P, 2, ENTRIES, 2], BF16, name="picked", align_bytes=64)
+        x_grouped = [keep.tile([P, HALF, 2, 2], BF16, name="x_grouped%d" % h, align_bytes=64) for h in range(2)]
+        x_codes = [keep.tile([P, HALF], U32, name="x_codes%d" % h, align_bytes=64) for h in range(2)]
+        x_scales = [keep.tile([P, HALF], U8, name="x_scales%d" % h, align_bytes=64) for h in range(2)]
+        w_grouped = [keep.tile([P, P, PACK], BF16, name="w_grouped%d" % c, align_bytes=64) for c in range(M_TILES)]
+        w_codes = [keep.tile([P, P], U32, name="w_codes%d" % c, align_bytes=64) for c in range(M_TILES)]
+        w_scales = [keep.tile([P, P], U8, name="w_scales%d" % c, align_bytes=64) for c in range(M_TILES)]
 
         def cast(i):
-            u, c0, c1, v = CHUNKS[i]
-            n = c1 - c0
-            if n > v:
-                nc.scalar.activation(
-                    pools_bf[u][:, c0 + v : c1, :], raws[i][:, :, v:n].rearrange("p t c -> p c t"), COPY
-                )
-            if v:
-                nc.vector.tensor_copy(
-                    out=pools_bf[u][:, c0 : c0 + v, :], in_=raws[i][:, :, 0:v].rearrange("p t c -> p c t")
-                )
+            u, first, end, by_vector = CHUNKS[i]
+            middle = first + by_vector
+            if middle < end:
+                source = x_raw[i][:, :, by_vector:].rearrange("p t n -> p n t")
+                nc.scalar.activation(window[u][:, middle:end, :], source, COPY)
+            if first < middle:
+                source = x_raw[i][:, :, :by_vector].rearrange("p t n -> p n t")
+                nc.vector.tensor_copy(out=window[u][:, first:middle, :], in_=source)
 
-        def gather(u, h):
-            window = pools_bf[u][:].rearrange("p c t -> p (c t)").bitcast(U32)
-            if h == 0:
-                words = gathered[0][:].rearrange("p c u t -> p (c u t)").bitcast(U32)
-                target = words.rearrange("p (c u) -> p c u", u=2)[:, :, u]
-            else:
-                target = plain[:, u, :, :].rearrange("p c t -> p (c t)").bitcast(U32)
-            a = h * (HALF // 16)
-            nc.vector.tensor_copy(out=target, in_=window.indirect(offsets[:, a : a + HALF // 16]))
+        def gather(u, first, end):
+            words = window[u][:].rearrange("p n t -> p (n t)").bitcast(U32)
+            target = picked[:, u, first:end, :].rearrange("p c t -> p (c t)").bitcast(U32)
+            nc.vector.tensor_copy(out=target, in_=words.indirect(offsets[:, first // LANES : end // LANES]))
 
-        cast(0)
-        cast(1)
-        gather(0, 0)
-        cast(2)
-        gather(0, 1)
-        cast(3)
-        cast(4)
-        def interleave_w(s):
-            nc.scalar.activation(
-                w_grouped[s][:].rearrange("p e m j -> p m j e"),
-                w_raws[s][:].rearrange("p j m e -> p m j e"),
-                COPY,
+        def group_x(q):
+            h, r = divmod(q, 2)
+            words_in = picked[:].rearrange("p u c t -> p (u c t)").bitcast(F32).rearrange("p (u c) -> p c u", u=2)
+            words_out = x_grouped[h][:].rearrange("p c u t -> p (c u t)").bitcast(F32).rearrange("p (c u) -> p c u", u=2)
+            nc.scalar.copy(
+                words_out[:, r * QUARTER : (r + 1) * QUARTER, :], words_in[:, q * QUARTER : (q + 1) * QUARTER, :]
             )
-
-        gather(1, 0)
-        gather(1, 1)
-        interleave_w(0)
-        nc.scalar.copy(gathered[1][:], plain[:].rearrange("p u c t -> p c u t"))
-        interleave_w(1)
 
         def quantize_x(h):
             nc.vector.quantize_mx(
-                out=codes[h][:].bitcast(FP8X4),
-                scales=scales[h][:],
-                in_=gathered[h][:].rearrange("p c u t -> p (c u t)"),
+                out=x_codes[h][:].bitcast(FP8X4),
+                scales=x_scales[h][:],
+                in_=x_grouped[h][:].rearrange("p c u t -> p (c u t)"),
             )
 
-        def quantize_w(s):
+        def w_tile(c):
+            return w_raw[c // 2][:, :, :, c % 2].rearrange("p j m -> p m j")
+
+        def quantize_w(c):
             nc.vector.quantize_mx(
-                out=w_codes[s][:].bitcast(FP8X4),
-                scales=w_scales[s][:],
-                in_=w_grouped[s][:].rearrange("p e m j -> p (e m j)"),
+                out=w_codes[c][:].bitcast(FP8X4),
+                scales=w_scales[c][:],
+                in_=w_grouped[c][:].rearrange("p m j -> p (m j)"),
             )
 
+        cast(0)
+        gather(0, 0, ENTRIES)
+        cast(1)
+        cast(2)
+        cast(3)
+        for q in range(4):
+            gather(1, q * QUARTER, (q + 1) * QUARTER)
+            group_x(q)
+        nc.gpsimd.tensor_scalar(out=w_grouped[0][:], in0=w_tile(0), scalar1=1.0, scalar2=0.0, op0=MULT, op1=ADD)
+        for c in range(1, M_TILES):
+            nc.scalar.activation(w_grouped[c][:], w_tile(c), COPY)
         quantize_w(0)
         quantize_x(0)
         quantize_x(1)
-        quantize_w(1)
+        for c in range(1, M_TILES):
+            quantize_w(c)
 
-        y_max = keep.tile([P, M_TILES, G], F32, name="y_max")
-        y_out = keep.tile([P, M_TILES, G], F32, name="y_out")
-        out_rows = out.rearrange("(s p e) g -> s p e g", s=W_HALVES, e=PAIR)
-        def product(t, h):
-            s, e = divmod(t, PAIR)
-            m_cols = slice(e * P, (e + 1) * P)
-            bank = psum.tile([P, HALF], F32, name="bank%d" % (2 * t + h))
+        largest = keep.tile([P, LAST, G], F32, name="largest")
+        result = keep.tile([P, M_TILES, G], F32, name="result")
+        out_rows = out.rearrange("(s p e) g -> p s e g", s=2, e=2)
+
+        def multiply(c, h):
+            bank = psum.tile([P, HALF], F32, name="bank%d" % (2 * c + h))
             nc.tensor.matmul_mx(
                 out=bank[:],
-                lhsT=w_codes[s][:, m_cols].bitcast(FP8X4),
-                lhsT_scale=w_scales[s][:, m_cols],
-                rhs=codes[h][:].bitcast(FP8X4),
-                rhs_scale=scales[h][:],
+                lhsT=w_codes[c][:].bitcast(FP8X4),
+                lhsT_scale=w_scales[c][:],
+                rhs=x_codes[h][:].bitcast(FP8X4),
+                rhs_scale=x_scales[h][:],
                 start=True,
                 stop=True,
             )
+            return bank
+
+        def keep_largest(target, source, h):
             nc.vector.tensor_reduce(
-                out=y_max[:, t, h * G_HALF : (h + 1) * G_HALF],
-                in_=bank[:].rearrange("p (g k) -> p g k", k=K),
+                out=target[:, h * G_HALF : (h + 1) * G_HALF],
+                in_=source[:].rearrange("p (g k) -> p g k", k=K),
                 axis=AXIS_X,
                 op=MAX,
             )
 
-        def finish(t):
-            s, e = divmod(t, PAIR)
-            nc.scalar.activation(y_out[:, t, :], y_max[:, t, :], IDENTITY, bias=bias_sb[:, s, e : e + 1])
-
-        product(0, 0)
-        product(1, 0)
-        product(0, 1)
-        product(1, 1)
-        finish(0)
-        finish(1)
-        nc.sync.dma_start(out=out_rows[0], in_=y_out[:, 0:2, :])
-        for t in (2, 3):
-            product(t, 0)
-            product(t, 1)
-            finish(t)
-            nc.sync.dma_start(out=out_rows[1, :, t - 2, :], in_=y_out[:, t, :])
+        for c in range(LAST):
+            s, e = divmod(c, 2)
+            for h in range(2):
+                keep_largest(largest[:, c, :], multiply(c, h), h)
+            nc.scalar.activation(result[:, c, :], largest[:, c, :], IDENTITY, bias=bias_sb[:, s, e : e + 1])
+            if c == 1:
+                nc.sync.dma_start(out=out_rows[:, 0], in_=result[:, 0:2, :])
+        nc.sync.dma_start(out=out_rows[:, 1, 0, :], in_=result[:, 2, :])
+        for h in range(2):
+            biased = keep.tile([P, HALF], F32, name="biased%d" % h)
+            nc.scalar.activation(biased[:], multiply(LAST, h)[:], IDENTITY, bias=bias_sb[:, 1, 1:2])
+            keep_largest(result[:, LAST, :], biased, h)
+        nc.sync.dma_start(out=out_rows[:, 1, 1, :], in_=result[:, LAST, :])

from contextlib import ExitStack

import concourse.mybir as mybir

F32 = mybir.dt.float32
BF16 = mybir.dt.bfloat16
U32 = mybir.dt.uint32
U16 = mybir.dt.uint16
U8 = mybir.dt.uint8
FP8X4 = mybir.dt.float8_e4m3fn_x4
COPY = mybir.ActivationFunctionType.Copy
IDENTITY = mybir.ActivationFunctionType.Identity
MAX = mybir.AluOpType.max
MULT = mybir.AluOpType.mult
ADD = mybir.AluOpType.add
AXIS_X = mybir.AxisListType.X

P = 128
D, T, M, G, K = 512, 2048, 512, 128, 8
ENTRIES = G * K
PACK = D // P
HALF = ENTRIES // 2
QUARTER = ENTRIES // 4
G_HALF = HALF // K
M_TILES = M // P
LAST = M_TILES - 1
LANES = 16

FLOPS = 2 * D * M * ENTRIES

CHUNKS = [
    (0, 0, 2048, 1344),
    (1, 0, 1024, 0),
    (1, 1024, 1664, 640),
    (1, 1664, 2048, 288),
]


def tile_attend_edge_bias_kernel(tc, xT, w, bias, offs, out):
    nc = tc.nc
    with ExitStack() as ctx:
        keep = ctx.enter_context(tc.tile_pool(name="keep", bufs=1))
        psum = ctx.enter_context(tc.psum_pool(name="psum", bufs=1))

        offsets = keep.tile([P, ENTRIES // LANES], U16, name="offsets")
        x_rows = xT.rearrange("(p u t) n -> u p t n", u=2, t=2)
        x_raw = []
        for i, (u, first, end, by_vector) in enumerate(CHUNKS):
            raw = keep.tile([P, 2, end - first], F32, name="x_raw%d" % i)
            nc.sync.dma_start(out=raw[:], in_=x_rows[u, :, :, first:end])
            x_raw.append(raw)
            if i == 0:
                nc.sync.dma_start(offsets[:], offs)
        w_rows = w.rearrange("(p j) (s m e) -> s p j m e", j=PACK, s=2, e=2)
        w_raw = []
        for s in range(2):
            raw = keep.tile([P, PACK, P, 2], F32, name="w_raw%d" % s)
            nc.sync.dma_start(out=raw[:], in_=w_rows[s])
            w_raw.append(raw)
        bias_sb = keep.tile([P, 2, 2], F32, name="bias_sb")
        nc.sync.dma_start(out=bias_sb[:], in_=bias.rearrange("(s p e) o -> p s (e o)", s=2, e=2))

        zeros = keep.tile([P, 8], F32, name="zeros")
        zeros_copy = keep.tile([P, 8], BF16, name="zeros_copy")
        nc.vector.memset(zeros[:], 0.0)
        nc.scalar.activation(zeros_copy[:], zeros[:], COPY)

        window = [keep.tile([P, T, 2], BF16, name="window%d" % u, align_bytes=64) for u in range(2)]
        picked = keep.tile([P, 2, ENTRIES, 2], BF16, name="picked", align_bytes=64)
        x_grouped = [keep.tile([P, HALF, 2, 2], BF16, name="x_grouped%d" % h, align_bytes=64) for h in range(2)]
        x_codes = [keep.tile([P, HALF], U32, name="x_codes%d" % h, align_bytes=64) for h in range(2)]
        x_scales = [keep.tile([P, HALF], U8, name="x_scales%d" % h, align_bytes=64) for h in range(2)]
        w_grouped = [keep.tile([P, P, PACK], BF16, name="w_grouped%d" % c, align_bytes=64) for c in range(M_TILES)]
        w_codes = [keep.tile([P, P], U32, name="w_codes%d" % c, align_bytes=64) for c in range(M_TILES)]
        w_scales = [keep.tile([P, P], U8, name="w_scales%d" % c, align_bytes=64) for c in range(M_TILES)]

        def cast(i):
            u, first, end, by_vector = CHUNKS[i]
            middle = first + by_vector
            if middle < end:
                source = x_raw[i][:, :, by_vector:].rearrange("p t n -> p n t")
                nc.scalar.activation(window[u][:, middle:end, :], source, COPY)
            if first < middle:
                source = x_raw[i][:, :, :by_vector].rearrange("p t n -> p n t")
                nc.vector.tensor_copy(out=window[u][:, first:middle, :], in_=source)

        def gather(u, first, end):
            words = window[u][:].rearrange("p n t -> p (n t)").bitcast(U32)
            target = picked[:, u, first:end, :].rearrange("p c t -> p (c t)").bitcast(U32)
            nc.vector.tensor_copy(out=target, in_=words.indirect(offsets[:, first // LANES : end // LANES]))

        def group_x(q):
            h, r = divmod(q, 2)
            words_in = picked[:].rearrange("p u c t -> p (u c t)").bitcast(F32).rearrange("p (u c) -> p c u", u=2)
            words_out = x_grouped[h][:].rearrange("p c u t -> p (c u t)").bitcast(F32).rearrange("p (c u) -> p c u", u=2)
            nc.scalar.copy(
                words_out[:, r * QUARTER : (r + 1) * QUARTER, :], words_in[:, q * QUARTER : (q + 1) * QUARTER, :]
            )

        def quantize_x(h):
            nc.vector.quantize_mx(
                out=x_codes[h][:].bitcast(FP8X4),
                scales=x_scales[h][:],
                in_=x_grouped[h][:].rearrange("p c u t -> p (c u t)"),
            )

        def w_tile(c):
            return w_raw[c // 2][:, :, :, c % 2].rearrange("p j m -> p m j")

        def quantize_w(c):
            nc.vector.quantize_mx(
                out=w_codes[c][:].bitcast(FP8X4),
                scales=w_scales[c][:],
                in_=w_grouped[c][:].rearrange("p m j -> p (m j)"),
            )

        cast(0)
        gather(0, 0, ENTRIES)
        cast(1)
        cast(2)
        cast(3)
        for q in range(4):
            gather(1, q * QUARTER, (q + 1) * QUARTER)
            group_x(q)
        nc.gpsimd.tensor_scalar(out=w_grouped[0][:], in0=w_tile(0), scalar1=1.0, scalar2=0.0, op0=MULT, op1=ADD)
        for c in range(1, M_TILES):
            nc.scalar.activation(w_grouped[c][:], w_tile(c), COPY)
        quantize_w(0)
        quantize_x(0)
        quantize_x(1)
        for c in range(1, M_TILES):
            quantize_w(c)

        largest = keep.tile([P, LAST, G], F32, name="largest")
        result = keep.tile([P, M_TILES, G], F32, name="result")
        out_rows = out.rearrange("(s p e) g -> p s e g", s=2, e=2)

        def multiply(c, h):
            bank = psum.tile([P, HALF], F32, name="bank%d" % (2 * c + h))
            nc.tensor.matmul_mx(
                out=bank[:],
                lhsT=w_codes[c][:].bitcast(FP8X4),
                lhsT_scale=w_scales[c][:],
                rhs=x_codes[h][:].bitcast(FP8X4),
                rhs_scale=x_scales[h][:],
                start=True,
                stop=True,
            )
            return bank

        def keep_largest(target, source, h):
            nc.vector.tensor_reduce(
                out=target[:, h * G_HALF : (h + 1) * G_HALF],
                in_=source[:].rearrange("p (g k) -> p g k", k=K),
                axis=AXIS_X,
                op=MAX,
            )

        for c in range(LAST):
            s, e = divmod(c, 2)
            for h in range(2):
                keep_largest(largest[:, c, :], multiply(c, h), h)
            nc.scalar.activation(result[:, c, :], largest[:, c, :], IDENTITY, bias=bias_sb[:, s, e : e + 1])
            if c == 1:
                nc.sync.dma_start(out=out_rows[:, 0], in_=result[:, 0:2, :])
        nc.sync.dma_start(out=out_rows[:, 1, 0, :], in_=result[:, 2, :])
        for h in range(2):
            biased = keep.tile([P, HALF], F32, name="biased%d" % h)
            nc.scalar.activation(biased[:], multiply(LAST, h)[:], IDENTITY, bias=bias_sb[:, 1, 1:2])
            keep_largest(result[:, LAST, :], biased, h)
        nc.sync.dma_start(out=out_rows[:, 1, 1, :], in_=result[:, LAST, :])
